import numpy as np
import ml_dtypes


def mxq(x, axis, fmt="e4m3"):
    dtype, down = {"e4m3": (ml_dtypes.float8_e4m3fn, 7), "e5m2": (ml_dtypes.float8_e5m2, 14)}[fmt]
    v = np.moveaxis(np.asarray(x, np.float32).astype(ml_dtypes.bfloat16).astype(np.float64), axis, -1)
    blocks = v.reshape(v.shape[:-1] + (-1, 32))
    amax = np.abs(blocks).max(-1, keepdims=True)
    byte = np.maximum(np.where(amax > 0, np.frexp(amax)[1] - 1 + 127, 0) - down, 1)
    scale = np.exp2(byte - 127.0)
    codes = (blocks / scale).astype(np.float32).astype(dtype).astype(np.float64)
    return np.moveaxis((codes * scale).reshape(v.shape), -1, axis)


WIDE = False


def mx_kscale(k):
    if not WIDE:
        return np.ones(k)
    levels = np.array([10, -10, 5, -5, 0])
    if k % 512:
        return np.exp2(np.random.permutation(np.resize(levels, k // 32))).repeat(32)
    a = np.empty((k // 512, 16))
    for p in range(k // 512):
        a[p, :8] = np.random.permutation(np.resize(levels, 8))
        for g in range(8):
            far = levels[np.abs(levels - a[p, g]) >= 10]
            a[p, g + 8] = far[np.random.randint(len(far))]
    return np.exp2(a.ravel()).repeat(32)


BF16 = ml_dtypes.bfloat16


def bf(x):
    return np.asarray(x, np.float32).astype(BF16)


def f64(x):
    return np.asarray(x).astype(np.float64)


E2M1 = np.array([0.0, 0.5, 1.0, 1.5, 2.0, 3.0, 4.0, 6.0, -0.0, -0.5, -1.0, -1.5, -2.0, -3.0, -4.0, -6.0])


def pack_weight(w, fmt):
    k, n = w.shape
    w = f64(bf(w)).reshape(k // 32, 32, n)
    amax = np.abs(w).max(1)
    if fmt == "e4m3":
        byte = np.frexp(amax)[1] - 1 + 127 - 7
    else:
        mant, ex = np.frexp(amax / 6.0)
        byte = np.where(mant > 0.5, ex, ex - 1) + 127
    byte = np.clip(np.where(amax > 0, byte, 1), 1, 254)
    scaled = (w * np.exp2(127.0 - byte)[:, None, :]).reshape(k, n).astype(np.float32)
    by_word = np.ascontiguousarray(scaled.reshape(k // 512, 128, 4, n).transpose(0, 1, 3, 2))
    if fmt == "e4m3":
        words = by_word.astype(ml_dtypes.float8_e4m3fn).view(np.uint8)
    else:
        c = by_word.astype(ml_dtypes.float4_e2m1fn).view(np.uint8) & 0xF
        words = c[..., 0::2] | (c[..., 1::2] << 4)
    return np.ascontiguousarray(words), np.ascontiguousarray(byte.astype(np.uint8).reshape(k // 512, 16, n))


def unpack_weight(words, scales, fmt):
    g, p, n, _ = words.shape
    if fmt == "e4m3":
        vals = np.ascontiguousarray(words).view(ml_dtypes.float8_e4m3fn).astype(np.float64)
    else:
        nib = np.empty((g, p, n, 4), np.uint8)
        nib[..., 0::2] = words & 0xF
        nib[..., 1::2] = words >> 4
        vals = E2M1[nib]
    vals = vals * np.repeat(np.exp2(scales.astype(np.float64) - 127.0), 8, axis=1)[..., None]
    return vals.transpose(0, 1, 3, 2).reshape(g * 512, n)
def pack4(w):
    words, scales = pack_weight(w, "e2m1")
    return words.reshape(words.shape[0], 128, -1), scales


def unpack4(words, scales):
    return unpack_weight(words.reshape(words.shape[0], 128, -1, 2), scales, "e2m1")


M, K, N, D, P = 1024, 1024, 2048, 512, 4


def setup_inputs():
    s = mx_kscale(K)
    x = np.random.standard_normal((M, K)) * s
    fields = 0.5 * np.random.standard_normal((K, N)) / np.sqrt(K) / s[:, None]
    gains = 0.6 * np.random.standard_normal((K, N)) / np.sqrt(K) / s[:, None]
    linear = np.random.standard_normal((K, D)) / np.sqrt(K) / s[:, None]
    field_words, field_scales = pack4(fields)
    gain_words, gain_scales = pack_weight(gains, "e4m3")
    return {"x": bf(x),
            "field_words": field_words, "field_scales": field_scales,
            "gain_words": gain_words, "gain_scales": gain_scales,
            "w_lin": bf(linear)}


def reference(x, field_words, field_scales, gain_words, gain_scales, w_lin):
    xq = mxq(f64(x), 1, "e4m3")
    drive = xq @ unpack4(field_words, field_scales)
    gain = xq @ unpack_weight(gain_words, gain_scales, "e4m3")
    direct = xq @ mxq(f64(w_lin), 0, "e4m3")
    votes = np.exp(drive) * gain
    pooled = votes.reshape(M, D, P).sum(axis=2)
    return pooled + direct

@@ -1,0 +1,292 @@
+from contextlib import ExitStack
+
+import concourse.mybir as mybir
+from concourse.masks import make_identity
+
+M, K, N, D, POOL = 1024, 1024, 2048, 512, 4
+FLOPS = 2 * M * K * (2 * N + D)
+
+F32 = mybir.dt.float32
+BF16 = mybir.dt.bfloat16
+U32 = mybir.dt.uint32
+I32 = mybir.dt.int32
+U8 = mybir.dt.uint8
+FP8X4 = mybir.dt.float8_e4m3fn_x4
+FP4X4 = mybir.dt.float4_e2m1fn_x4
+ADD = mybir.AluOpType.add
+MULT = mybir.AluOpType.mult
+EXP = mybir.ActivationFunctionType.Exp
+
+P = 128
+G = K // 512
+MT = M // P
+NT = 512
+NB = N // NT
+WARM = 4
+
+
+def tile_rate_pool_readout_s10_kernel(
+    tc, x, field_words, field_scales, gain_words, gain_scales, w_lin, out
+):
+    nc = tc.nc
+    with ExitStack() as ctx:
+        keep = ctx.enter_context(tc.tile_pool(name="keep", bufs=1))
+        work = ctx.enter_context(tc.tile_pool(name="work", bufs=2))
+        psum = ctx.enter_context(tc.psum_pool(name="psum", bufs=1))
+        ctx.enter_context(tc.manual_schedule())
+
+        x_rows = x.rearrange("(m p) k -> p m k", p=P)
+        x_sb = [keep.tile([P, 1, K], BF16, name="x_sb%d" % i, align_bytes=64) for i in range(2)]
+        x_sb += [keep.tile([P, 2, K], BF16, name="x_sb%d" % i, align_bytes=64) for i in range(2, 5)]
+        x_codes = keep.tile([P, MT, G, P], U32, name="x_codes", align_bytes=64)
+        x_scales = keep.tile([P, MT, G, P], U8, name="x_scales", align_bytes=64)
+        f_words = [keep.tile([P, G, 2 * NT], U8, name="f_words0", align_bytes=64),
+                   keep.tile([P, G, 2 * (N - NT)], U8, name="f_words1", align_bytes=64)]
+        f_scales = [keep.tile([P, G, NT], U8, name="f_scales0", align_bytes=64),
+                    keep.tile([P, G, N - NT], U8, name="f_scales1", align_bytes=64)]
+        g_words = [keep.tile([P, G, 4 * NT], U8, name="g_words%d" % n, align_bytes=64) for n in range(NB)]
+        g_scales = [keep.tile([P, G, NT], U8, name="g_scales0", align_bytes=64),
+                    keep.tile([P, G, N - NT], U8, name="g_scales1", align_bytes=64)]
+        l_raw = keep.tile([P, G, 4, D], BF16, name="l_raw", align_bytes=64)
+        l_grp = keep.tile([P, G, D, 4], BF16, name="l_grp", align_bytes=64)
+        l_codes = keep.tile([P, G, D], U32, name="l_codes", align_bytes=64)
+        l_scales = keep.tile([P, G, D], U8, name="l_scales", align_bytes=64)
+        votes = [keep.tile([P, N], F32, name="votes%d" % m, align_bytes=64) for m in range(MT)]
+        ident = keep.tile([P, P], F32, name="ident", align_bytes=64)
+        zeros = keep.tile([P, NT], BF16, name="zeros", align_bytes=64)
+        warm = keep.tile([P, 1], F32, name="warm", align_bytes=64)
+
+        gw = gain_words.rearrange("g p n t -> p g (n t)")
+        fw = field_words.rearrange("g p b -> p g b")
+        fs = field_scales.rearrange("g r n -> r g n")
+        gs = gain_scales.rearrange("g r n -> r g n")
+
+        def load_words(tile, src, lo, hi):
+            nc.sync.dma_start(out=tile[:].bitcast(I32), in_=src[:, :, lo:hi].bitcast(I32))
+
+        def load_scales(tile, src, lo, hi):
+            for q in range(4):
+                nc.sync.dma_start(out=tile[32 * q : 32 * q + 4, :, :].bitcast(I32),
+                                  in_=src[4 * q : 4 * q + 4, :, lo:hi].bitcast(I32))
+
+        nc.vector.memset(zeros[:], 0.0)
+        nc.vector.memset(f_scales[0][:].bitcast(I32), 0)
+        nc.vector.memset(g_scales[0][:].bitcast(I32), 0)
+        nc.vector.memset(warm[:], 0.0)
+        nc.vector.memset(f_scales[1][:].bitcast(I32), 0)
+        nc.vector.memset(g_scales[1][:].bitcast(I32), 0)
+        make_identity(nc, ident[:])
+        nc.scalar.activation(out=warm[:], in_=warm[:], func=EXP)
+
+        nc.sync.dma_start(out=x_sb[0][:], in_=x_rows[:, 0:1, :])
+        nc.sync.dma_start(out=x_sb[1][:], in_=x_rows[:, 1:2, :])
+        load_words(f_words[0], fw, 0, 2 * NT)
+        load_scales(f_scales[0], fs, 0, NT)
+        load_words(g_words[0], gw, 0, 4 * NT)
+        load_scales(g_scales[0], gs, 0, NT)
+        nc.sync.dma_start(out=x_sb[2][:], in_=x_rows[:, 2:4, :])
+        l_view = w_lin.rearrange("(g p j) w -> p g j w", g=G, j=4)
+        for g in range(G):
+            nc.sync.dma_start(out=l_raw[:, g, :, :], in_=l_view[:, g, :, :])
+        load_scales(f_scales[1], fs, NT, N)
+        load_scales(g_scales[1], gs, NT, N)
+        load_words(f_words[1], fw, 2 * NT, 2 * N)
+        for n in range(1, NB):
+            load_words(g_words[n], gw, 4 * NT * n, 4 * NT * (n + 1))
+        nc.sync.dma_start(out=x_sb[3][:], in_=x_rows[:, 4:6, :])
+        nc.sync.dma_start(out=x_sb[4][:], in_=x_rows[:, 6:8, :])
+
+        def x_words(m):
+            if m < 2:
+                return x_sb[m][:, 0, :].bitcast(F32)
+            return x_sb[1 + m // 2][:, m % 2, :].bitcast(F32)
+
+        def psum_tile(tag, bufs, shape):
+            return psum.tile(shape, F32, name="ps_" + tag, tag=tag, bufs=bufs)
+
+        def transpose(m, g, bank):
+            for u in range(2):
+                nc.tensor.transpose(bank[:, u, :], x_words(m)[:, 256 * g + u : 256 * (g + 1) : 2], ident[:])
+
+        grouped = {}
+        banks = {}
+
+        def transpose_all(m):
+            tag = "turn" if m < 4 else ("drive" if m % 2 == 0 else "gain")
+            bank = psum_tile(tag, 2 if m < 4 else 3, [P, G, 2, P])
+            for g in range(G):
+                transpose(m, g, bank[:, g, :, :])
+            banks[m] = bank
+
+        def copy_words(m, engine):
+            pair = m // 2
+            if pair not in grouped:
+                grouped[pair] = work.tile([P, 2, G, P, 4], BF16, name="grouped", tag="grouped", align_bytes=64)
+            dst = grouped[pair][:, m % 2, :, :, :].bitcast(F32)
+            engine(out=dst, in_=banks[m][:].rearrange("p g u r -> p g r u"))
+
+        def quantize(m0, count):
+            src = grouped[m0 // 2][:, m0 % 2 : m0 % 2 + count, :, :, :]
+            nc.vector.quantize_mx(
+                out=x_codes[:, m0 : m0 + count, :, :].rearrange("p m g r -> p (m g r)").bitcast(FP8X4),
+                scales=x_scales[:, m0 : m0 + count, :, :].rearrange("p m g r -> p (m g r)"),
+                in_=src.rearrange("p m g r t -> p (m g r t)"))
+
+        def group_linear(i):
+            g, c = divmod(i, 4)
+            cols = slice(128 * c, 128 * (c + 1))
+            nc.scalar.copy(out=l_grp[:, g, cols, :], in_=l_raw[:, g, :, cols].rearrange("p j w -> p w j"))
+
+        def quantize_linear(g):
+            nc.vector.quantize_mx(
+                out=l_codes[:, g, :].bitcast(FP8X4), scales=l_scales[:, g, :],
+                in_=l_grp[:, g, :, :].rearrange("p w j -> p (w j)"))
+
+        def field(n, g):
+            if n == 0:
+                return f_words[0][:, g, :].bitcast(FP4X4), f_scales[0][:, g, :]
+            c = (n - 1) * NT
+            return f_words[1][:, g, 2 * c : 2 * (c + NT)].bitcast(FP4X4), f_scales[1][:, g, c : c + NT]
+
+        def gain(n, g):
+            if n == 0:
+                return g_words[0][:, g, :].bitcast(FP8X4), g_scales[0][:, g, :]
+            c = (n - 1) * NT
+            return g_words[n][:, g, :].bitcast(FP8X4), g_scales[1][:, g, c : c + NT]
+
+        def product(bank, m, operand):
+            for g in range(G):
+                codes, scales = operand(g)
+                nc.tensor.matmul_mx(
+                    out=bank, lhsT=x_codes[:, m, g, :].bitcast(FP8X4), lhsT_scale=x_scales[:, m, g, :],
+                    rhs=codes, rhs_scale=scales, start=(g == 0), stop=(g == G - 1))
+
+        def block(m, n):
+            drive_bank = psum_tile("drive", 3, [P, NT])
+            product(drive_bank[:], m, lambda g: field(n, g))
+            gain_bank = psum_tile("gain", 3, [P, NT])
+            product(gain_bank[:], m, lambda g: gain(n, g))
+            rate = work.tile([P, NT], F32, name="rate", tag="rate", bufs=4, align_bytes=64)
+            nc.scalar.activation(out=rate[:], in_=drive_bank[:], func=EXP)
+            nc.vector.tensor_tensor(out=votes[m][:, NT * n : NT * (n + 1)], in0=gain_bank[:], in1=rate[:], op=MULT)
+
+        direct_banks = {}
+
+        def direct(m):
+            bank = psum_tile("turn", 2, [P, D])
+            product(bank[:], m, lambda g: (l_codes[:, g, :].bitcast(FP8X4), l_scales[:, g, :]))
+            direct_banks[m] = bank
+
+        halves = {}
+        results = {}
+
+        def add_pairs(m, lo, hi):
+            if m not in halves:
+                halves[m] = work.tile([P, D, 2], F32, name="halves", tag="halves", bufs=4, align_bytes=64)
+            v = votes[m][:].rearrange("p (d j) -> p d j", j=POOL)
+            nc.vector.tensor_tensor(out=halves[m][:, lo:hi, :], in0=v[:, lo:hi, 0:2], in1=v[:, lo:hi, 2:4], op=ADD)
+
+        def add_halves(m, lo, hi):
+            if m not in results:
+                results[m] = work.tile([P, 2, D], F32, name="result", tag="result", bufs=3, align_bytes=64)
+            nc.vector.tensor_tensor(out=results[m][:, 0, lo:hi], in0=halves[m][:, lo:hi, 0], in1=halves[m][:, lo:hi, 1], op=ADD)
+
+        def add_direct(m, lo, hi):
+            nc.vector.tensor_tensor(out=results[m][:, 1, lo:hi], in0=direct_banks[m][:, lo:hi], in1=results[m][:, 0, lo:hi], op=ADD)
+            nc.sync.dma_start(out=out[P * m : P * (m + 1), lo:hi], in_=results[m][:, 1, lo:hi])
+
+        idle = psum_tile("drive", 3, [P, NT])
+        for i in range(WARM):
+            nc.tensor.matmul(idle[:], lhsT=zeros[:, 0:P], rhs=zeros[:], start=True, stop=True)
+        bank_a = psum_tile("turn", 2, [P, 2, P])
+        transpose(0, 0, bank_a[:])
+        bank_b = psum_tile("gain", 3, [P, 2, P])
+        transpose(0, 1, bank_b[:])
+        grouped[0] = work.tile([P, 2, G, P, 4], BF16, name="grouped", tag="grouped", align_bytes=64)
+        nc.vector.tensor_copy(out=grouped[0][:, 0, 0, :, :].bitcast(F32), in_=bank_a[:].rearrange("p u r -> p r u"))
+        nc.scalar.copy(out=grouped[0][:, 0, 1, :, :].bitcast(F32), in_=bank_b[:].rearrange("p u r -> p r u"))
+        for g in range(G):
+            nc.vector.quantize_mx(
+                out=x_codes[:, 0, g, :].bitcast(FP8X4), scales=x_scales[:, 0, g, :],
+                in_=grouped[0][:, 0, g, :, :].rearrange("p r t -> p (r t)"))
+        transpose_all(1)
+        copy_words(1, nc.scalar.copy)
+        quantize(1, 1)
+
+        pending = []
+
+        def pop():
+            if pending:
+                pending.pop(0)()
+
+        def after_block(m, n):
+            if (m, n) == (0, 0):
+                transpose_all(2)
+                transpose_all(3)
+                copy_words(2, nc.scalar.copy)
+                copy_words(3, nc.scalar.copy)
+                quantize(2, 2)
+            if n == 0 and m in (1, 2):
+                group_linear(2 * m - 2)
+                group_linear(2 * m - 1)
+            if n > 0 and m == 0 or (m, n) == (1, 1):
+                group_linear(4 + (n - 1 if m == 0 else 3))
+            if (m, n) == (0, 1):
+                quantize_linear(0)
+            if (m, n) == (1, 2):
+                quantize_linear(1)
+            for first in (4, 6):
+                if (m, n) == ((2, 3) if first == 4 else (5, 0)):
+                    transpose_all(first)
+                    transpose_all(first + 1)
+                    copy_words(first, nc.scalar.copy)
+                    copy_words(first + 1, nc.scalar.copy)
+                    quantize(first, 2)
+            if n == 0 and m < 4:
+                pending.append(lambda: add_pairs(m, 0, 128))
+            if m >= 4 and n == 1:
+                pending.append(lambda: add_pairs(m, 0, 256))
+            if n == 3:
+                if m < 4:
+                    pending.append(lambda: add_pairs(m, 128, 512))
+                else:
+                    pending.append(lambda: add_pairs(m, 256, 512))
+                pending.append(lambda: add_halves(m, 0, 512))
+            if (m, n) == (1, 3):
+                direct(0)
+                direct(1)
+                pending.insert(0, lambda: add_direct(0, 0, 512))
+                pending.append(lambda: add_direct(1, 0, 512))
+            elif n == 3 and m > 1:
+                direct(m)
+                pending.append(lambda: add_direct(m, 0, 512))
+            pop()
+
+        for m in range(4):
+            block(m, 0)
+            after_block(m, 0)
+        for m in range(4):
+            for n in range(1, NB):
+                block(m, n)
+                after_block(m, n)
+        for m in range(4, MT - 1):
+            for n in range(NB):
+                block(m, n)
+                after_block(m, n)
+        last = MT - 1
+        for n in range(NB - 1):
+            block(last, n)
+            if n == 1:
+                pending.append(lambda: add_pairs(last, 0, 256))
+            if n == 2:
+                direct(last)
+            pop()
+        while pending:
+            pop()
+        add_pairs(last, 256, 384)
+        block(last, 3)
+        add_halves(last, 0, 384)
+        add_pairs(last, 384, 512)
+        add_direct(last, 0, 384)
+        add_halves(last, 384, 512)
+        add_direct(last, 384, 512)

@@ -42,11 +42,9 @@ def tile_rate_pool_readout_s10_kernel(
         x_scales = keep.tile([P, MT, G, P], U8, name="x_scales", align_bytes=64)
         f_words = [keep.tile([P, G, 2 * NT], U8, name="f_words0", align_bytes=64),
                    keep.tile([P, G, 2 * (N - NT)], U8, name="f_words1", align_bytes=64)]
-        f_scales = [keep.tile([P, G, NT], U8, name="f_scales0", align_bytes=64),
-                    keep.tile([P, G, N - NT], U8, name="f_scales1", align_bytes=64)]
+        f_scales = keep.tile([P, G, N], U8, name="f_scales", align_bytes=64)
         g_words = [keep.tile([P, G, 4 * NT], U8, name="g_words%d" % n, align_bytes=64) for n in range(NB)]
-        g_scales = [keep.tile([P, G, NT], U8, name="g_scales0", align_bytes=64),
-                    keep.tile([P, G, N - NT], U8, name="g_scales1", align_bytes=64)]
+        g_scales = keep.tile([P, G, N], U8, name="g_scales", align_bytes=64)
         l_raw = keep.tile([P, G, 4, D], BF16, name="l_raw", align_bytes=64)
         l_grp = keep.tile([P, G, D, 4], BF16, name="l_grp", align_bytes=64)
         l_codes = keep.tile([P, G, D], U32, name="l_codes", align_bytes=64)
@@ -64,32 +62,28 @@ def tile_rate_pool_readout_s10_kernel(
         def load_words(tile, src, lo, hi):
             nc.sync.dma_start(out=tile[:].bitcast(I32), in_=src[:, :, lo:hi].bitcast(I32))
 
-        def load_scales(tile, src, lo, hi):
+        def load_scales(tile, src):
             for q in range(4):
                 nc.sync.dma_start(out=tile[32 * q : 32 * q + 4, :, :].bitcast(I32),
-                                  in_=src[4 * q : 4 * q + 4, :, lo:hi].bitcast(I32))
+                                  in_=src[4 * q : 4 * q + 4, :, :].bitcast(I32))
 
-        nc.vector.memset(zeros[:], 0.0)
-        nc.vector.memset(f_scales[0][:].bitcast(I32), 0)
-        nc.vector.memset(g_scales[0][:].bitcast(I32), 0)
+        nc.vector.memset(f_scales[:].bitcast(I32), 0)
         nc.vector.memset(warm[:], 0.0)
-        nc.vector.memset(f_scales[1][:].bitcast(I32), 0)
-        nc.vector.memset(g_scales[1][:].bitcast(I32), 0)
+        nc.vector.memset(g_scales[:].bitcast(I32), 0)
+        nc.gpsimd.memset(zeros[:], 0.0)
         make_identity(nc, ident[:])
         nc.scalar.activation(out=warm[:], in_=warm[:], func=EXP)
 
         nc.sync.dma_start(out=x_sb[0][:], in_=x_rows[:, 0:1, :])
         nc.sync.dma_start(out=x_sb[1][:], in_=x_rows[:, 1:2, :])
         load_words(f_words[0], fw, 0, 2 * NT)
-        load_scales(f_scales[0], fs, 0, NT)
+        load_scales(f_scales, fs)
         load_words(g_words[0], gw, 0, 4 * NT)
-        load_scales(g_scales[0], gs, 0, NT)
-        nc.sync.dma_start(out=x_sb[2][:], in_=x_rows[:, 2:4, :])
+        load_scales(g_scales, gs)
+        nc.gpsimd.dma_start(out=x_sb[2][:], in_=x_rows[:, 2:4, :])
         l_view = w_lin.rearrange("(g p j) w -> p g j w", g=G, j=4)
         for g in range(G):
             nc.sync.dma_start(out=l_raw[:, g, :, :], in_=l_view[:, g, :, :])
-        load_scales(f_scales[1], fs, NT, N)
-        load_scales(g_scales[1], gs, NT, N)
         load_words(f_words[1], fw, 2 * NT, 2 * N)
         for n in range(1, NB):
             load_words(g_words[n], gw, 4 * NT * n, 4 * NT * (n + 1))
@@ -104,9 +98,19 @@ def tile_rate_pool_readout_s10_kernel(
         def psum_tile(tag, bufs, shape):
             return psum.tile(shape, F32, name="ps_" + tag, tag=tag, bufs=bufs)
 
+        split = {}
+
+        def split_words(m):
+            split[m] = work.tile([P, G, 2, P], F32, name="split", tag="split", bufs=2, align_bytes=64)
+            nc.scalar.copy(out=split[m][:], in_=x_words(m).rearrange("p (g i u) -> p g u i", g=G, u=2))
+
         def transpose(m, g, bank):
             for u in range(2):
-                nc.tensor.transpose(bank[:, u, :], x_words(m)[:, 256 * g + u : 256 * (g + 1) : 2], ident[:])
+                if m in split:
+                    src = split[m][:, g, u, :]
+                else:
+                    src = x_words(m)[:, 256 * g + u : 256 * (g + 1) : 2]
+                nc.tensor.transpose(bank[:, u, :], src, ident[:])
 
         grouped = {}
         banks = {}
@@ -135,7 +139,8 @@ def tile_rate_pool_readout_s10_kernel(
         def group_linear(i):
             g, c = divmod(i, 4)
             cols = slice(128 * c, 128 * (c + 1))
-            nc.scalar.copy(out=l_grp[:, g, cols, :], in_=l_raw[:, g, :, cols].rearrange("p j w -> p w j"))
+            engine = nc.vector.tensor_copy if i in (1, 3, 5) else nc.scalar.copy
+            engine(out=l_grp[:, g, cols, :], in_=l_raw[:, g, :, cols].rearrange("p j w -> p w j"))
 
         def quantize_linear(g):
             nc.vector.quantize_mx(
@@ -143,16 +148,14 @@ def tile_rate_pool_readout_s10_kernel(
                 in_=l_grp[:, g, :, :].rearrange("p w j -> p (w j)"))
 
         def field(n, g):
+            scales = f_scales[:, g, NT * n : NT * (n + 1)]
             if n == 0:
-                return f_words[0][:, g, :].bitcast(FP4X4), f_scales[0][:, g, :]
+                return f_words[0][:, g, :].bitcast(FP4X4), scales
             c = (n - 1) * NT
-            return f_words[1][:, g, 2 * c : 2 * (c + NT)].bitcast(FP4X4), f_scales[1][:, g, c : c + NT]
+            return f_words[1][:, g, 2 * c : 2 * (c + NT)].bitcast(FP4X4), scales
 
         def gain(n, g):
-            if n == 0:
-                return g_words[0][:, g, :].bitcast(FP8X4), g_scales[0][:, g, :]
-            c = (n - 1) * NT
-            return g_words[n][:, g, :].bitcast(FP8X4), g_scales[1][:, g, c : c + NT]
+            return g_words[n][:, g, :].bitcast(FP8X4), g_scales[:, g, NT * n : NT * (n + 1)]
 
         def product(bank, m, operand):
             for g in range(G):
@@ -161,14 +164,22 @@ def tile_rate_pool_readout_s10_kernel(
                     out=bank, lhsT=x_codes[:, m, g, :].bitcast(FP8X4), lhsT_scale=x_scales[:, m, g, :],
                     rhs=codes, rhs_scale=scales, start=(g == 0), stop=(g == G - 1))
 
+        rates = {}
+
+        def drive(m, n):
+            bank = psum_tile("drive", 3, [P, NT])
+            product(bank[:], m, lambda g: field(n, g))
+            rates[m, n] = work.tile([P, NT], F32, name="rate", tag="rate", bufs=4, align_bytes=64)
+            nc.scalar.activation(out=rates[m, n][:], in_=bank[:], func=EXP)
+
+        def vote(m, n):
+            bank = psum_tile("gain", 3, [P, NT])
+            product(bank[:], m, lambda g: gain(n, g))
+            nc.vector.tensor_tensor(out=votes[m][:, NT * n : NT * (n + 1)], in0=bank[:], in1=rates[m, n][:], op=MULT)
+
         def block(m, n):
-            drive_bank = psum_tile("drive", 3, [P, NT])
-            product(drive_bank[:], m, lambda g: field(n, g))
-            gain_bank = psum_tile("gain", 3, [P, NT])
-            product(gain_bank[:], m, lambda g: gain(n, g))
-            rate = work.tile([P, NT], F32, name="rate", tag="rate", bufs=4, align_bytes=64)
-            nc.scalar.activation(out=rate[:], in_=drive_bank[:], func=EXP)
-            nc.vector.tensor_tensor(out=votes[m][:, NT * n : NT * (n + 1)], in0=gain_bank[:], in1=rate[:], op=MULT)
+            drive(m, n)
+            vote(m, n)
 
         direct_banks = {}
 
@@ -186,10 +197,10 @@ def tile_rate_pool_readout_s10_kernel(
             v = votes[m][:].rearrange("p (d j) -> p d j", j=POOL)
             nc.vector.tensor_tensor(out=halves[m][:, lo:hi, :], in0=v[:, lo:hi, 0:2], in1=v[:, lo:hi, 2:4], op=ADD)
 
-        def add_halves(m, lo, hi):
+        def add_halves(m, lo, hi, engine=nc.gpsimd):
             if m not in results:
                 results[m] = work.tile([P, 2, D], F32, name="result", tag="result", bufs=3, align_bytes=64)
-            nc.vector.tensor_tensor(out=results[m][:, 0, lo:hi], in0=halves[m][:, lo:hi, 0], in1=halves[m][:, lo:hi, 1], op=ADD)
+            engine.tensor_tensor(out=results[m][:, 0, lo:hi], in0=halves[m][:, lo:hi, 0], in1=halves[m][:, lo:hi, 1], op=ADD)
 
         def add_direct(m, lo, hi):
             nc.vector.tensor_tensor(out=results[m][:, 1, lo:hi], in0=direct_banks[m][:, lo:hi], in1=results[m][:, 0, lo:hi], op=ADD)
@@ -198,95 +209,113 @@ def tile_rate_pool_readout_s10_kernel(
         idle = psum_tile("drive", 3, [P, NT])
         for i in range(WARM):
             nc.tensor.matmul(idle[:], lhsT=zeros[:, 0:P], rhs=zeros[:], start=True, stop=True)
-        bank_a = psum_tile("turn", 2, [P, 2, P])
-        transpose(0, 0, bank_a[:])
-        bank_b = psum_tile("gain", 3, [P, 2, P])
-        transpose(0, 1, bank_b[:])
         grouped[0] = work.tile([P, 2, G, P, 4], BF16, name="grouped", tag="grouped", align_bytes=64)
-        nc.vector.tensor_copy(out=grouped[0][:, 0, 0, :, :].bitcast(F32), in_=bank_a[:].rearrange("p u r -> p r u"))
-        nc.scalar.copy(out=grouped[0][:, 0, 1, :, :].bitcast(F32), in_=bank_b[:].rearrange("p u r -> p r u"))
-        for g in range(G):
-            nc.vector.quantize_mx(
-                out=x_codes[:, 0, g, :].bitcast(FP8X4), scales=x_scales[:, 0, g, :],
-                in_=grouped[0][:, 0, g, :, :].rearrange("p r t -> p (r t)"))
-        transpose_all(1)
-        copy_words(1, nc.scalar.copy)
-        quantize(1, 1)
 
-        pending = []
+        def first_tile(m):
+            copies = (nc.vector.tensor_copy, nc.scalar.copy)
+            for g in range(G):
+                bank = psum_tile("turn" if g == 0 else "gain", 2 if g == 0 else 3, [P, 2, P])
+                transpose(m, g, bank[:])
+                copies[g](out=grouped[0][:, m, g, :, :].bitcast(F32), in_=bank[:].rearrange("p u r -> p r u"))
+            for g in range(G):
+                nc.vector.quantize_mx(
+                    out=x_codes[:, m, g, :].bitcast(FP8X4), scales=x_scales[:, m, g, :],
+                    in_=grouped[0][:, m, g, :, :].rearrange("p r t -> p (r t)"))
 
-        def pop():
-            if pending:
-                pending.pop(0)()
-
-        def after_block(m, n):
-            if (m, n) == (0, 0):
-                transpose_all(2)
-                transpose_all(3)
-                copy_words(2, nc.scalar.copy)
-                copy_words(3, nc.scalar.copy)
-                quantize(2, 2)
-            if n == 0 and m in (1, 2):
-                group_linear(2 * m - 2)
-                group_linear(2 * m - 1)
-            if n > 0 and m == 0 or (m, n) == (1, 1):
-                group_linear(4 + (n - 1 if m == 0 else 3))
-            if (m, n) == (0, 1):
-                quantize_linear(0)
-            if (m, n) == (1, 2):
-                quantize_linear(1)
-            for first in (4, 6):
-                if (m, n) == ((2, 3) if first == 4 else (5, 0)):
-                    transpose_all(first)
-                    transpose_all(first + 1)
-                    copy_words(first, nc.scalar.copy)
-                    copy_words(first + 1, nc.scalar.copy)
-                    quantize(first, 2)
-            if n == 0 and m < 4:
-                pending.append(lambda: add_pairs(m, 0, 128))
-            if m >= 4 and n == 1:
-                pending.append(lambda: add_pairs(m, 0, 256))
-            if n == 3:
-                if m < 4:
-                    pending.append(lambda: add_pairs(m, 128, 512))
-                else:
-                    pending.append(lambda: add_pairs(m, 256, 512))
-                pending.append(lambda: add_halves(m, 0, 512))
-            if (m, n) == (1, 3):
-                direct(0)
-                direct(1)
-                pending.insert(0, lambda: add_direct(0, 0, 512))
-                pending.append(lambda: add_direct(1, 0, 512))
-            elif n == 3 and m > 1:
-                direct(m)
-                pending.append(lambda: add_direct(m, 0, 512))
-            pop()
-
-        for m in range(4):
+        first_tile(0)
+        nc.tensor.matmul(idle[:], lhsT=zeros[:, 0:P], rhs=zeros[:], start=True, stop=True)
+        first_tile(1)
+        drive(0, 0)
+        drive(1, 0)
+        transpose_all(2)
+        transpose_all(3)
+        copy_words(2, nc.scalar.copy)
+        copy_words(3, nc.vector.tensor_copy)
+        quantize(2, 1)
+        quantize(3, 1)
+        vote(0, 0)
+        vote(1, 0)
+        add_pairs(0, 0, 128)
+        for m in (2, 3):
             block(m, 0)
-            after_block(m, 0)
+            group_linear(2 * m - 4)
+            group_linear(2 * m - 3)
+            add_pairs(m - 1, 0, 128)
         for m in range(4):
             for n in range(1, NB):
                 block(m, n)
-                after_block(m, n)
-        for m in range(4, MT - 1):
+                if (m, n) == (0, 1):
+                    add_pairs(3, 0, 128)
+                if m == 0 and n < 3:
+                    group_linear(2 + 2 * n)
+                    group_linear(3 + 2 * n)
+                if m == 0 and n > 1:
+                    quantize_linear(n - 2)
+                if (m, n) == (2, 1):
+                    split_words(4)
+                if (m, n) == (2, 2):
+                    split_words(5)
+                if (m, n) == (3, 1):
+                    transpose_all(4)
+                    transpose_all(5)
+                    copy_words(4, nc.scalar.copy)
+                    copy_words(5, nc.scalar.copy)
+                if (m, n) == (3, 2):
+                    quantize(4, 2)
+                if m > 0 and n == 1:
+                    add_pairs(m - 1, 128, 512)
+                    add_halves(m - 1, 0, 512)
+                if m > 0 and n == 2:
+                    direct(m - 1)
+                if m > 0 and n == 3:
+                    add_direct(m - 1, 0, 512)
+        last = MT - 1
+        for m in range(4, last):
             for n in range(NB):
                 block(m, n)
-                after_block(m, n)
-        last = MT - 1
-        for n in range(NB - 1):
-            block(last, n)
-            if n == 1:
-                pending.append(lambda: add_pairs(last, 0, 256))
-            if n == 2:
-                direct(last)
-            pop()
-        while pending:
-            pop()
+                if n == 0:
+                    add_pairs(m - 1, 128 if m == 4 else 256, 512)
+                    add_halves(m - 1, 0, 512)
+                    direct(m - 1)
+                if (m, n) == (4, 1):
+                    split_words(6)
+                if (m, n) == (4, 2):
+                    split_words(7)
+                if (m, n) == (5, 0):
+                    transpose_all(6)
+                    transpose_all(7)
+                    copy_words(6, nc.scalar.copy)
+                    copy_words(7, nc.scalar.copy)
+                if (m, n) == (5, 1):
+                    quantize(6, 2)
+                if n == 2:
+                    add_direct(m - 1, 0, 512)
+                    add_pairs(m, 0, 256)
+        block(last, 0)
+        add_pairs(last - 1, 256, 512)
+        add_halves(last - 1, 0, 512)
+        block(last, 1)
+        direct(last - 1)
+        direct(last)
+        add_pairs(last, 0, 256)
+        add_halves(last, 0, 256)
+        add_direct(last - 1, 0, 512)
+        block(last, 2)
+        add_direct(last, 0, 256)
         add_pairs(last, 256, 384)
-        block(last, 3)
-        add_halves(last, 0, 384)
-        add_pairs(last, 384, 512)
-        add_direct(last, 0, 384)
-        add_halves(last, 384, 512)
+        add_halves(last, 256, 384, nc.vector)
+        drive(last, 3)
+        half = NT // 2
+        for h in range(2):
+            bank = psum_tile("gain", 3, [P, half])
+            cols = slice(half * h, half * (h + 1))
+            product(bank[:], last, lambda g: (gain(3, g)[0][:, cols], gain(3, g)[1][:, cols]))
+            lo = NT * 3 + half * h
+            nc.vector.tensor_tensor(out=votes[last][:, lo : lo + half], in0=bank[:], in1=rates[last, 3][:, cols], op=MULT)
+            if h == 0:
+                add_direct(last, 256, 384)
+        for h in range(2):
+            add_pairs(last, 384 + 64 * h, 448 + 64 * h)
+        for h in range(2):
+            add_halves(last, 384 + 64 * h, 448 + 64 * h, nc.vector)
         add_direct(last, 384, 512)

@@ -40,11 +40,12 @@ def tile_rate_pool_readout_s10_kernel(
         x_sb += [keep.tile([P, 2, K], BF16, name="x_sb%d" % i, align_bytes=64) for i in range(2, 5)]
         x_codes = keep.tile([P, MT, G, P], U32, name="x_codes", align_bytes=64)
         x_scales = keep.tile([P, MT, G, P], U8, name="x_scales", align_bytes=64)
-        f_words = [keep.tile([P, G, 2 * NT], U8, name="f_words0", align_bytes=64),
-                   keep.tile([P, G, 2 * (N - NT)], U8, name="f_words1", align_bytes=64)]
-        f_scales = keep.tile([P, G, N], U8, name="f_scales", align_bytes=64)
+        f_words = [keep.tile([P, G, 2 * NT], U8, name="f_words%d" % n, align_bytes=64) for n in range(NB)]
+        f_scales = [keep.tile([P, G, NT], U8, name="f_scales0", align_bytes=64),
+                    keep.tile([P, G, N - NT], U8, name="f_scales1", align_bytes=64)]
         g_words = [keep.tile([P, G, 4 * NT], U8, name="g_words%d" % n, align_bytes=64) for n in range(NB)]
-        g_scales = keep.tile([P, G, N], U8, name="g_scales", align_bytes=64)
+        g_scales = [keep.tile([P, G, NT], U8, name="g_scales0", align_bytes=64),
+                    keep.tile([P, G, N - NT], U8, name="g_scales1", align_bytes=64)]
         l_raw = keep.tile([P, G, 4, D], BF16, name="l_raw", align_bytes=64)
         l_grp = keep.tile([P, G, D, 4], BF16, name="l_grp", align_bytes=64)
         l_codes = keep.tile([P, G, D], U32, name="l_codes", align_bytes=64)
@@ -62,33 +63,37 @@ def tile_rate_pool_readout_s10_kernel(
         def load_words(tile, src, lo, hi):
             nc.sync.dma_start(out=tile[:].bitcast(I32), in_=src[:, :, lo:hi].bitcast(I32))
 
-        def load_scales(tile, src):
+        def load_scales(tile, src, lo, hi):
             for q in range(4):
                 nc.sync.dma_start(out=tile[32 * q : 32 * q + 4, :, :].bitcast(I32),
-                                  in_=src[4 * q : 4 * q + 4, :, :].bitcast(I32))
+                                  in_=src[4 * q : 4 * q + 4, :, lo:hi].bitcast(I32))
 
-        nc.vector.memset(f_scales[:].bitcast(I32), 0)
+        nc.vector.memset(f_scales[0][:].bitcast(I32), 0)
         nc.vector.memset(warm[:], 0.0)
-        nc.vector.memset(g_scales[:].bitcast(I32), 0)
+        nc.vector.memset(g_scales[0][:].bitcast(I32), 0)
+        nc.vector.memset(f_scales[1][:].bitcast(I32), 0)
+        nc.vector.memset(g_scales[1][:].bitcast(I32), 0)
         nc.gpsimd.memset(zeros[:], 0.0)
         make_identity(nc, ident[:])
         nc.scalar.activation(out=warm[:], in_=warm[:], func=EXP)
 
         nc.sync.dma_start(out=x_sb[0][:], in_=x_rows[:, 0:1, :])
+        load_scales(f_scales[0], fs, 0, NT)
         nc.sync.dma_start(out=x_sb[1][:], in_=x_rows[:, 1:2, :])
         load_words(f_words[0], fw, 0, 2 * NT)
-        load_scales(f_scales, fs)
         load_words(g_words[0], gw, 0, 4 * NT)
-        load_scales(g_scales, gs)
-        nc.gpsimd.dma_start(out=x_sb[2][:], in_=x_rows[:, 2:4, :])
+        load_scales(g_scales[0], gs, 0, NT)
+        for i in (2, 3):
+            nc.sync.dma_start(out=x_sb[i][:], in_=x_rows[:, 2 * i - 2 : 2 * i, :])
+        load_scales(f_scales[1], fs, NT, N)
+        load_scales(g_scales[1], gs, NT, N)
+        nc.sync.dma_start(out=x_sb[4][:], in_=x_rows[:, 6:8, :])
         l_view = w_lin.rearrange("(g p j) w -> p g j w", g=G, j=4)
         for g in range(G):
             nc.sync.dma_start(out=l_raw[:, g, :, :], in_=l_view[:, g, :, :])
-        load_words(f_words[1], fw, 2 * NT, 2 * N)
         for n in range(1, NB):
+            load_words(f_words[n], fw, 2 * NT * n, 2 * NT * (n + 1))
             load_words(g_words[n], gw, 4 * NT * n, 4 * NT * (n + 1))
-        nc.sync.dma_start(out=x_sb[3][:], in_=x_rows[:, 4:6, :])
-        nc.sync.dma_start(out=x_sb[4][:], in_=x_rows[:, 6:8, :])
 
         def x_words(m):
             if m < 2:
@@ -98,26 +103,15 @@ def tile_rate_pool_readout_s10_kernel(
         def psum_tile(tag, bufs, shape):
             return psum.tile(shape, F32, name="ps_" + tag, tag=tag, bufs=bufs)
 
-        split = {}
-
-        def split_words(m):
-            split[m] = work.tile([P, G, 2, P], F32, name="split", tag="split", bufs=2, align_bytes=64)
-            nc.scalar.copy(out=split[m][:], in_=x_words(m).rearrange("p (g i u) -> p g u i", g=G, u=2))
-
         def transpose(m, g, bank):
             for u in range(2):
-                if m in split:
-                    src = split[m][:, g, u, :]
-                else:
-                    src = x_words(m)[:, 256 * g + u : 256 * (g + 1) : 2]
-                nc.tensor.transpose(bank[:, u, :], src, ident[:])
+                nc.tensor.transpose(bank[:, u, :], x_words(m)[:, 256 * g + u : 256 * (g + 1) : 2], ident[:])
 
         grouped = {}
         banks = {}
 
         def transpose_all(m):
-            tag = "turn" if m < 4 else ("drive" if m % 2 == 0 else "gain")
-            bank = psum_tile(tag, 2 if m < 4 else 3, [P, G, 2, P])
+            bank = psum_tile("turn", 2, [P, G, 2, P])
             for g in range(G):
                 transpose(m, g, bank[:, g, :, :])
             banks[m] = bank
@@ -139,7 +133,7 @@ def tile_rate_pool_readout_s10_kernel(
         def group_linear(i):
             g, c = divmod(i, 4)
             cols = slice(128 * c, 128 * (c + 1))
-            engine = nc.vector.tensor_copy if i in (1, 3, 5) else nc.scalar.copy
+            engine = nc.vector.tensor_copy if i == 3 else nc.scalar.copy
             engine(out=l_grp[:, g, cols, :], in_=l_raw[:, g, :, cols].rearrange("p j w -> p w j"))
 
         def quantize_linear(g):
@@ -147,15 +141,16 @@ def tile_rate_pool_readout_s10_kernel(
                 out=l_codes[:, g, :].bitcast(FP8X4), scales=l_scales[:, g, :],
                 in_=l_grp[:, g, :, :].rearrange("p w j -> p (w j)"))
 
-        def field(n, g):
-            scales = f_scales[:, g, NT * n : NT * (n + 1)]
+        def scale_cols(tiles, n, g):
             if n == 0:
-                return f_words[0][:, g, :].bitcast(FP4X4), scales
-            c = (n - 1) * NT
-            return f_words[1][:, g, 2 * c : 2 * (c + NT)].bitcast(FP4X4), scales
+                return tiles[0][:, g, :]
+            return tiles[1][:, g, NT * (n - 1) : NT * n]
+
+        def field(n, g):
+            return f_words[n][:, g, :].bitcast(FP4X4), scale_cols(f_scales, n, g)
 
         def gain(n, g):
-            return g_words[n][:, g, :].bitcast(FP8X4), g_scales[:, g, NT * n : NT * (n + 1)]
+            return g_words[n][:, g, :].bitcast(FP8X4), scale_cols(g_scales, n, g)
 
         def product(bank, m, operand):
             for g in range(G):
@@ -193,13 +188,13 @@ def tile_rate_pool_readout_s10_kernel(
 
         def add_pairs(m, lo, hi):
             if m not in halves:
-                halves[m] = work.tile([P, D, 2], F32, name="halves", tag="halves", bufs=4, align_bytes=64)
+                halves[m] = work.tile([P, D, 2], F32, name="halves", tag="halves", bufs=8, align_bytes=64)
             v = votes[m][:].rearrange("p (d j) -> p d j", j=POOL)
             nc.vector.tensor_tensor(out=halves[m][:, lo:hi, :], in0=v[:, lo:hi, 0:2], in1=v[:, lo:hi, 2:4], op=ADD)
 
-        def add_halves(m, lo, hi, engine=nc.gpsimd):
+        def add_halves(m, lo, hi, engine=nc.vector):
             if m not in results:
-                results[m] = work.tile([P, 2, D], F32, name="result", tag="result", bufs=3, align_bytes=64)
+                results[m] = work.tile([P, 2, D], F32, name="result", tag="result", bufs=8, align_bytes=64)
             engine.tensor_tensor(out=results[m][:, 0, lo:hi], in0=halves[m][:, lo:hi, 0], in1=halves[m][:, lo:hi, 1], op=ADD)
 
         def add_direct(m, lo, hi):
@@ -230,80 +225,67 @@ def tile_rate_pool_readout_s10_kernel(
         transpose_all(2)
         transpose_all(3)
         copy_words(2, nc.scalar.copy)
-        copy_words(3, nc.vector.tensor_copy)
         quantize(2, 1)
+        copy_words(3, nc.vector.tensor_copy)
         quantize(3, 1)
         vote(0, 0)
         vote(1, 0)
         add_pairs(0, 0, 128)
-        for m in (2, 3):
+        for m in range(2, MT):
             block(m, 0)
-            group_linear(2 * m - 4)
-            group_linear(2 * m - 3)
+            if m in (2, 4):
+                transpose_all(m + 2)
+                transpose_all(m + 3)
+                copy_words(m + 2, nc.scalar.copy)
+                quantize(m + 2, 1)
+                copy_words(m + 3, nc.scalar.copy)
+                quantize(m + 3, 1)
+            if m >= 5:
+                group_linear(m - 5)
+            if m == 7:
+                group_linear(3)
             add_pairs(m - 1, 0, 128)
-        for m in range(4):
-            for n in range(1, NB):
-                block(m, n)
-                if (m, n) == (0, 1):
-                    add_pairs(3, 0, 128)
-                if m == 0 and n < 3:
-                    group_linear(2 + 2 * n)
-                    group_linear(3 + 2 * n)
-                if m == 0 and n > 1:
-                    quantize_linear(n - 2)
-                if (m, n) == (2, 1):
-                    split_words(4)
-                if (m, n) == (2, 2):
-                    split_words(5)
-                if (m, n) == (3, 1):
-                    transpose_all(4)
-                    transpose_all(5)
-                    copy_words(4, nc.scalar.copy)
-                    copy_words(5, nc.scalar.copy)
-                if (m, n) == (3, 2):
-                    quantize(4, 2)
-                if m > 0 and n == 1:
-                    add_pairs(m - 1, 128, 512)
-                    add_halves(m - 1, 0, 512)
-                if m > 0 and n == 2:
-                    direct(m - 1)
-                if m > 0 and n == 3:
-                    add_direct(m - 1, 0, 512)
+            add_halves(m - 2, 0, 128)
         last = MT - 1
-        for m in range(4, last):
-            for n in range(NB):
-                block(m, n)
-                if n == 0:
-                    add_pairs(m - 1, 128 if m == 4 else 256, 512)
-                    add_halves(m - 1, 0, 512)
-                    direct(m - 1)
-                if (m, n) == (4, 1):
-                    split_words(6)
-                if (m, n) == (4, 2):
-                    split_words(7)
-                if (m, n) == (5, 0):
-                    transpose_all(6)
-                    transpose_all(7)
-                    copy_words(6, nc.scalar.copy)
-                    copy_words(7, nc.scalar.copy)
-                if (m, n) == (5, 1):
-                    quantize(6, 2)
-                if n == 2:
-                    add_direct(m - 1, 0, 512)
-                    add_pairs(m, 0, 256)
-        block(last, 0)
-        add_pairs(last - 1, 256, 512)
-        add_halves(last - 1, 0, 512)
+        for m in range(last):
+            block(m, 1)
+            if m == 0:
+                quantize_linear(0)
+                add_pairs(last, 0, 128)
+                add_halves(last - 1, 0, 128)
+                group_linear(4)
+                group_linear(5)
+            else:
+                add_pairs(m - 1, 128, 512)
+            if m == 1:
+                quantize_linear(1)
+            if m == 2:
+                direct(0)
+            block(m, 2)
+            if m == 0:
+                add_halves(last, 0, 128)
+                group_linear(6)
+                group_linear(7)
+            else:
+                add_halves(m - 1, 128, 512)
+            if m == 2:
+                add_direct(0, 0, 512)
+            if m > 1:
+                direct(m - 1)
+            block(m, 3)
+            if m > 1:
+                add_direct(m - 1, 0, 512)
+            if m == last - 1:
+                add_pairs(m, 128, 384)
         block(last, 1)
+        add_pairs(last - 1, 384, 512)
         direct(last - 1)
-        direct(last)
-        add_pairs(last, 0, 256)
-        add_halves(last, 0, 256)
-        add_direct(last - 1, 0, 512)
+        add_halves(last - 1, 128, 512)
         block(last, 2)
-        add_direct(last, 0, 256)
-        add_pairs(last, 256, 384)
-        add_halves(last, 256, 384, nc.vector)
+        direct(last)
+        add_direct(last - 1, 0, 512)
+        add_pairs(last, 128, 384)
+        add_halves(last, 128, 384)
         drive(last, 3)
         half = NT // 2
         for h in range(2):
@@ -313,7 +295,7 @@ def tile_rate_pool_readout_s10_kernel(
             lo = NT * 3 + half * h
             nc.vector.tensor_tensor(out=votes[last][:, lo : lo + half], in0=bank[:], in1=rates[last, 3][:, cols], op=MULT)
             if h == 0:
-                add_direct(last, 256, 384)
+                add_direct(last, 0, 384)
         for h in range(2):
             add_pairs(last, 384 + 64 * h, 448 + 64 * h)
         for h in range(2):

@@ -23,6 +23,7 @@ MT = M // P
 NT = 512
 NB = N // NT
 WARM = 4
+EAGER = 6
 
 
 def tile_rate_pool_readout_s10_kernel(
@@ -50,7 +51,7 @@ def tile_rate_pool_readout_s10_kernel(
         l_grp = keep.tile([P, G, D, 4], BF16, name="l_grp", align_bytes=64)
         l_codes = keep.tile([P, G, D], U32, name="l_codes", align_bytes=64)
         l_scales = keep.tile([P, G, D], U8, name="l_scales", align_bytes=64)
-        votes = [keep.tile([P, N], F32, name="votes%d" % m, align_bytes=64) for m in range(MT)]
+        votes = [keep.tile([P, NB, POOL, P], F32, name="votes%d" % m, align_bytes=64) for m in range(MT)]
         ident = keep.tile([P, P], F32, name="ident", align_bytes=64)
         zeros = keep.tile([P, NT], BF16, name="zeros", align_bytes=64)
         warm = keep.tile([P, 1], F32, name="warm", align_bytes=64)
@@ -164,13 +165,14 @@ def tile_rate_pool_readout_s10_kernel(
         def drive(m, n):
             bank = psum_tile("drive", 3, [P, NT])
             product(bank[:], m, lambda g: field(n, g))
-            rates[m, n] = work.tile([P, NT], F32, name="rate", tag="rate", bufs=4, align_bytes=64)
-            nc.scalar.activation(out=rates[m, n][:], in_=bank[:], func=EXP)
+            rates[m, n] = work.tile([P, POOL, P], F32, name="rate", tag="rate", bufs=4, align_bytes=64)
+            nc.scalar.activation(out=rates[m, n][:], in_=bank[:].rearrange("p (d j) -> p j d", j=POOL), func=EXP)
 
         def vote(m, n):
             bank = psum_tile("gain", 3, [P, NT])
             product(bank[:], m, lambda g: gain(n, g))
-            nc.vector.tensor_tensor(out=votes[m][:, NT * n : NT * (n + 1)], in0=bank[:], in1=rates[m, n][:], op=MULT)
+            nc.vector.tensor_tensor(out=votes[m][:, n, :, :], in0=bank[:].rearrange("p (d j) -> p j d", j=POOL),
+                                    in1=rates[m, n][:], op=MULT)
 
         def block(m, n):
             drive(m, n)
@@ -186,20 +188,23 @@ def tile_rate_pool_readout_s10_kernel(
         halves = {}
         results = {}
 
-        def add_pairs(m, lo, hi):
+        def add_pairs(m, lo, hi, d=slice(0, P)):
             if m not in halves:
-                halves[m] = work.tile([P, D, 2], F32, name="halves", tag="halves", bufs=8, align_bytes=64)
-            v = votes[m][:].rearrange("p (d j) -> p d j", j=POOL)
-            nc.vector.tensor_tensor(out=halves[m][:, lo:hi, :], in0=v[:, lo:hi, 0:2], in1=v[:, lo:hi, 2:4], op=ADD)
+                halves[m] = work.tile([P, NB, 2, P], F32, name="halves", tag="halves", bufs=8, align_bytes=64)
+            v = votes[m][:, lo:hi, :, d]
+            nc.vector.tensor_tensor(out=halves[m][:, lo:hi, :, d], in0=v[:, :, 0:2, :], in1=v[:, :, 2:4, :], op=ADD)
 
-        def add_halves(m, lo, hi, engine=nc.vector):
+        def add_halves(m, lo, hi, d=slice(0, P)):
             if m not in results:
-                results[m] = work.tile([P, 2, D], F32, name="result", tag="result", bufs=8, align_bytes=64)
-            engine.tensor_tensor(out=results[m][:, 0, lo:hi], in0=halves[m][:, lo:hi, 0], in1=halves[m][:, lo:hi, 1], op=ADD)
+                results[m] = work.tile([P, 2, NB, P], F32, name="result", tag="result", bufs=8, align_bytes=64)
+            h = halves[m][:, lo:hi, :, d]
+            nc.vector.tensor_tensor(out=results[m][:, 0, lo:hi, d], in0=h[:, :, 0, :], in1=h[:, :, 1, :], op=ADD)
 
         def add_direct(m, lo, hi):
-            nc.vector.tensor_tensor(out=results[m][:, 1, lo:hi], in0=direct_banks[m][:, lo:hi], in1=results[m][:, 0, lo:hi], op=ADD)
-            nc.sync.dma_start(out=out[P * m : P * (m + 1), lo:hi], in_=results[m][:, 1, lo:hi])
+            cols = slice(P * lo, P * hi)
+            pooled, total = [results[m][:, i, lo:hi, :].rearrange("p n d -> p (n d)") for i in (0, 1)]
+            nc.vector.tensor_tensor(out=total, in0=direct_banks[m][:, cols], in1=pooled, op=ADD)
+            nc.sync.dma_start(out=out[P * m : P * (m + 1), cols], in_=total)
 
         idle = psum_tile("drive", 3, [P, NT])
         for i in range(WARM):
@@ -230,7 +235,7 @@ def tile_rate_pool_readout_s10_kernel(
         quantize(3, 1)
         vote(0, 0)
         vote(1, 0)
-        add_pairs(0, 0, 128)
+        add_pairs(0, 0, 1)
         for m in range(2, MT):
             block(m, 0)
             if m in (2, 4):
@@ -244,60 +249,50 @@ def tile_rate_pool_readout_s10_kernel(
                 group_linear(m - 5)
             if m == 7:
                 group_linear(3)
-            add_pairs(m - 1, 0, 128)
-            add_halves(m - 2, 0, 128)
+            add_pairs(m - 1, 0, 1)
+            add_halves(m - 2, 0, 1)
         last = MT - 1
         for m in range(last):
             block(m, 1)
             if m == 0:
                 quantize_linear(0)
-                add_pairs(last, 0, 128)
-                add_halves(last - 1, 0, 128)
+                add_pairs(last, 0, 1)
+                add_halves(last - 1, 0, 1)
                 group_linear(4)
                 group_linear(5)
             else:
-                add_pairs(m - 1, 128, 512)
+                add_pairs(m - 1, 3 if m > EAGER else 1, 4)
             if m == 1:
                 quantize_linear(1)
             if m == 2:
                 direct(0)
             block(m, 2)
             if m == 0:
-                add_halves(last, 0, 128)
+                add_halves(last, 0, 1)
                 group_linear(6)
                 group_linear(7)
             else:
-                add_halves(m - 1, 128, 512)
+                add_halves(m - 1, 1, 4)
             if m == 2:
-                add_direct(0, 0, 512)
+                add_direct(0, 0, 4)
             if m > 1:
                 direct(m - 1)
             block(m, 3)
             if m > 1:
-                add_direct(m - 1, 0, 512)
-            if m == last - 1:
-                add_pairs(m, 128, 384)
+                add_direct(m - 1, 0, 4)
+            if m >= EAGER:
+                add_pairs(m, 1, 3)
         block(last, 1)
-        add_pairs(last - 1, 384, 512)
+        add_pairs(last - 1, 3, 4)
         direct(last - 1)
-        add_halves(last - 1, 128, 512)
+        add_halves(last - 1, 1, 4)
         block(last, 2)
         direct(last)
-        add_direct(last - 1, 0, 512)
-        add_pairs(last, 128, 384)
-        add_halves(last, 128, 384)
-        drive(last, 3)
-        half = NT // 2
-        for h in range(2):
-            bank = psum_tile("gain", 3, [P, half])
-            cols = slice(half * h, half * (h + 1))
-            product(bank[:], last, lambda g: (gain(3, g)[0][:, cols], gain(3, g)[1][:, cols]))
-            lo = NT * 3 + half * h
-            nc.vector.tensor_tensor(out=votes[last][:, lo : lo + half], in0=bank[:], in1=rates[last, 3][:, cols], op=MULT)
-            if h == 0:
-                add_direct(last, 0, 384)
-        for h in range(2):
-            add_pairs(last, 384 + 64 * h, 448 + 64 * h)
-        for h in range(2):
-            add_halves(last, 384 + 64 * h, 448 + 64 * h, nc.vector)
-        add_direct(last, 384, 512)
+        add_direct(last - 1, 0, 4)
+        add_pairs(last, 1, 3)
+        block(last, 3)
+        add_halves(last, 1, 3)
+        add_pairs(last, 3, 4)
+        add_direct(last, 0, 3)
+        add_halves(last, 3, 4)
+        add_direct(last, 3, 4)

@@ -51,7 +51,9 @@ def tile_rate_pool_readout_s10_kernel(
         l_grp = keep.tile([P, G, D, 4], BF16, name="l_grp", align_bytes=64)
         l_codes = keep.tile([P, G, D], U32, name="l_codes", align_bytes=64)
         l_scales = keep.tile([P, G, D], U8, name="l_scales", align_bytes=64)
-        votes = [keep.tile([P, NB, POOL, P], F32, name="votes%d" % m, align_bytes=64) for m in range(MT)]
+        votes = [keep.tile([P, 2, NB, POOL, P], F32, name="votes%d" % i, align_bytes=64) for i in range(MT // 2)]
+        halves = [keep.tile([P, 2, NB, 2, P], F32, name="halves%d" % i, align_bytes=64) for i in range(MT // 2)]
+        results = [keep.tile([P, 2, 2, NB, P], F32, name="results%d" % i, align_bytes=64) for i in range(MT // 2)]
         ident = keep.tile([P, P], F32, name="ident", align_bytes=64)
         zeros = keep.tile([P, NT], BF16, name="zeros", align_bytes=64)
         warm = keep.tile([P, 1], F32, name="warm", align_bytes=64)
@@ -83,15 +85,15 @@ def tile_rate_pool_readout_s10_kernel(
         nc.sync.dma_start(out=x_sb[1][:], in_=x_rows[:, 1:2, :])
         load_words(f_words[0], fw, 0, 2 * NT)
         load_words(g_words[0], gw, 0, 4 * NT)
+        nc.sync.dma_start(out=x_sb[2][:], in_=x_rows[:, 2:4, :])
         load_scales(g_scales[0], gs, 0, NT)
-        for i in (2, 3):
+        for i in (3, 4):
             nc.sync.dma_start(out=x_sb[i][:], in_=x_rows[:, 2 * i - 2 : 2 * i, :])
+        l_view = w_lin.rearrange("(g p j) w -> p g j w", g=G, j=4)
+        nc.sync.dma_start(out=l_raw[:, 0, :, :], in_=l_view[:, 0, :, :])
         load_scales(f_scales[1], fs, NT, N)
         load_scales(g_scales[1], gs, NT, N)
-        nc.sync.dma_start(out=x_sb[4][:], in_=x_rows[:, 6:8, :])
-        l_view = w_lin.rearrange("(g p j) w -> p g j w", g=G, j=4)
-        for g in range(G):
-            nc.sync.dma_start(out=l_raw[:, g, :, :], in_=l_view[:, g, :, :])
+        nc.sync.dma_start(out=l_raw[:, 1, :, :], in_=l_view[:, 1, :, :])
         for n in range(1, NB):
             load_words(f_words[n], fw, 2 * NT * n, 2 * NT * (n + 1))
             load_words(g_words[n], gw, 4 * NT * n, 4 * NT * (n + 1))
@@ -134,8 +136,7 @@ def tile_rate_pool_readout_s10_kernel(
         def group_linear(i):
             g, c = divmod(i, 4)
             cols = slice(128 * c, 128 * (c + 1))
-            engine = nc.vector.tensor_copy if i == 3 else nc.scalar.copy
-            engine(out=l_grp[:, g, cols, :], in_=l_raw[:, g, :, cols].rearrange("p j w -> p w j"))
+            nc.scalar.copy(out=l_grp[:, g, cols, :], in_=l_raw[:, g, :, cols].rearrange("p j w -> p w j"))
 
         def quantize_linear(g):
             nc.vector.quantize_mx(
@@ -171,7 +172,7 @@ def tile_rate_pool_readout_s10_kernel(
         def vote(m, n):
             bank = psum_tile("gain", 3, [P, NT])
             product(bank[:], m, lambda g: gain(n, g))
-            nc.vector.tensor_tensor(out=votes[m][:, n, :, :], in0=bank[:].rearrange("p (d j) -> p j d", j=POOL),
+            nc.vector.tensor_tensor(out=votes[m // 2][:, m % 2, n, :, :], in0=bank[:].rearrange("p (d j) -> p j d", j=POOL),
                                     in1=rates[m, n][:], op=MULT)
 
         def block(m, n):
@@ -185,26 +186,39 @@ def tile_rate_pool_readout_s10_kernel(
             product(bank[:], m, lambda g: (l_codes[:, g, :].bitcast(FP8X4), l_scales[:, g, :]))
             direct_banks[m] = bank
 
-        halves = {}
-        results = {}
+        def pooled_and_total(m, lo, hi):
+            return [results[m // 2][:, i, m % 2, lo:hi, :].rearrange("p n d -> p (n d)") for i in (0, 1)]
 
-        def add_pairs(m, lo, hi, d=slice(0, P)):
-            if m not in halves:
-                halves[m] = work.tile([P, NB, 2, P], F32, name="halves", tag="halves", bufs=8, align_bytes=64)
-            v = votes[m][:, lo:hi, :, d]
-            nc.vector.tensor_tensor(out=halves[m][:, lo:hi, :, d], in0=v[:, :, 0:2, :], in1=v[:, :, 2:4, :], op=ADD)
+        def store(m, lo, hi):
+            cols = slice(P * lo, P * hi)
+            nc.sync.dma_start(out=out[P * m : P * (m + 1), cols], in_=pooled_and_total(m, lo, hi)[1])
 
-        def add_halves(m, lo, hi, d=slice(0, P)):
-            if m not in results:
-                results[m] = work.tile([P, 2, NB, P], F32, name="result", tag="result", bufs=8, align_bytes=64)
-            h = halves[m][:, lo:hi, :, d]
-            nc.vector.tensor_tensor(out=results[m][:, 0, lo:hi, d], in0=h[:, :, 0, :], in1=h[:, :, 1, :], op=ADD)
+        direct_sb = {}
+
+        def copy_direct(m):
+            direct_sb[m] = work.tile([P, D], F32, name="direct_sb", tag="direct_sb", align_bytes=64)
+            nc.scalar.copy(out=direct_sb[m][:], in_=direct_banks[m][:])
+
+        def add_copied_direct(m):
+            pooled, total = pooled_and_total(m, 0, NB)
+            nc.gpsimd.tensor_tensor(out=total, in0=direct_sb[m][:], in1=pooled, op=ADD)
+            store(m, 0, NB)
+
+        def add_pairs(m, lo, hi, count=1):
+            ms = slice(m % 2, m % 2 + count)
+            v = votes[m // 2][:, ms, lo:hi, :, :].rearrange("p m n j d -> p m n (j d)")
+            h = halves[m // 2][:, ms, lo:hi, :, :].rearrange("p m n j d -> p m n (j d)")
+            nc.vector.tensor_tensor(out=h, in0=v[:, :, :, 0 : 2 * P], in1=v[:, :, :, 2 * P : 4 * P], op=ADD)
+
+        def add_halves(m, lo, hi, count=1):
+            ms = slice(m % 2, m % 2 + count)
+            h = halves[m // 2][:, ms, lo:hi, :, :]
+            nc.vector.tensor_tensor(out=results[m // 2][:, 0, ms, lo:hi, :], in0=h[:, :, :, 0, :], in1=h[:, :, :, 1, :], op=ADD)
 
         def add_direct(m, lo, hi):
-            cols = slice(P * lo, P * hi)
-            pooled, total = [results[m][:, i, lo:hi, :].rearrange("p n d -> p (n d)") for i in (0, 1)]
-            nc.vector.tensor_tensor(out=total, in0=direct_banks[m][:, cols], in1=pooled, op=ADD)
-            nc.sync.dma_start(out=out[P * m : P * (m + 1), cols], in_=total)
+            pooled, total = pooled_and_total(m, lo, hi)
+            nc.vector.tensor_tensor(out=total, in0=direct_banks[m][:, P * lo : P * hi], in1=pooled, op=ADD)
+            store(m, lo, hi)
 
         idle = psum_tile("drive", 3, [P, NT])
         for i in range(WARM):
@@ -231,11 +245,10 @@ def tile_rate_pool_readout_s10_kernel(
         transpose_all(3)
         copy_words(2, nc.scalar.copy)
         quantize(2, 1)
-        copy_words(3, nc.vector.tensor_copy)
+        copy_words(3, nc.scalar.copy)
         quantize(3, 1)
         vote(0, 0)
         vote(1, 0)
-        add_pairs(0, 0, 1)
         for m in range(2, MT):
             block(m, 0)
             if m in (2, 4):
@@ -245,42 +258,49 @@ def tile_rate_pool_readout_s10_kernel(
                 quantize(m + 2, 1)
                 copy_words(m + 3, nc.scalar.copy)
                 quantize(m + 3, 1)
-            if m >= 5:
-                group_linear(m - 5)
-            if m == 7:
-                group_linear(3)
-            add_pairs(m - 1, 0, 1)
-            add_halves(m - 2, 0, 1)
+            if m >= 4:
+                group_linear(m - 4)
+            if m % 2 == 0:
+                add_pairs(m - 2, 0, 1, 2)
+            else:
+                add_halves(m - 3, 0, 1, 2)
         last = MT - 1
         for m in range(last):
             block(m, 1)
             if m == 0:
-                quantize_linear(0)
-                add_pairs(last, 0, 1)
-                add_halves(last - 1, 0, 1)
+                add_pairs(last - 1, 0, 1, 2)
                 group_linear(4)
                 group_linear(5)
             else:
-                add_pairs(m - 1, 3 if m > EAGER else 1, 4)
+                add_pairs(m - 1, 1, 4)
+            if m > 2:
+                add_halves(m - 1, 1, 4)
+                direct(m - 1)
+                copy_direct(m - 1)
+                add_copied_direct(m - 1)
+            block(m, 2)
+            if m == 2:
+                direct(0)
+                copy_direct(0)
+                add_copied_direct(0)
+            if m == 0:
+                add_halves(last - 1, 0, 1, 2)
+                quantize_linear(0)
+                group_linear(6)
             if m == 1:
                 quantize_linear(1)
             if m == 2:
-                direct(0)
-            block(m, 2)
-            if m == 0:
-                add_halves(last, 0, 1)
-                group_linear(6)
-                group_linear(7)
-            else:
                 add_halves(m - 1, 1, 4)
-            if m == 2:
-                add_direct(0, 0, 4)
-            if m > 1:
-                direct(m - 1)
             block(m, 3)
-            if m > 1:
-                add_direct(m - 1, 0, 4)
-            if m >= EAGER:
+            if m == 0:
+                group_linear(7)
+            if m == 1:
+                add_halves(0, 1, 4)
+            if m == 2:
+                direct(1)
+                copy_direct(1)
+                add_copied_direct(1)
+            if m == last - 1:
                 add_pairs(m, 1, 3)
         block(last, 1)
         add_pairs(last - 1, 3, 4)

from contextlib import ExitStack

import concourse.mybir as mybir
from concourse.masks import make_identity

M, K, N, D, POOL = 1024, 1024, 2048, 512, 4
FLOPS = 2 * M * K * (2 * N + D)

F32 = mybir.dt.float32
BF16 = mybir.dt.bfloat16
U32 = mybir.dt.uint32
I32 = mybir.dt.int32
U8 = mybir.dt.uint8
FP8X4 = mybir.dt.float8_e4m3fn_x4
FP4X4 = mybir.dt.float4_e2m1fn_x4
ADD = mybir.AluOpType.add
MULT = mybir.AluOpType.mult
EXP = mybir.ActivationFunctionType.Exp

P = 128
G = K // 512
MT = M // P
NT = 512
NB = N // NT
WARM = 4
EAGER = 6


def tile_rate_pool_readout_s10_kernel(
    tc, x, field_words, field_scales, gain_words, gain_scales, w_lin, out
):
    nc = tc.nc
    with ExitStack() as ctx:
        keep = ctx.enter_context(tc.tile_pool(name="keep", bufs=1))
        work = ctx.enter_context(tc.tile_pool(name="work", bufs=2))
        psum = ctx.enter_context(tc.psum_pool(name="psum", bufs=1))
        ctx.enter_context(tc.manual_schedule())

        x_rows = x.rearrange("(m p) k -> p m k", p=P)
        x_sb = [keep.tile([P, 1, K], BF16, name="x_sb%d" % i, align_bytes=64) for i in range(2)]
        x_sb += [keep.tile([P, 2, K], BF16, name="x_sb%d" % i, align_bytes=64) for i in range(2, 5)]
        x_codes = keep.tile([P, MT, G, P], U32, name="x_codes", align_bytes=64)
        x_scales = keep.tile([P, MT, G, P], U8, name="x_scales", align_bytes=64)
        f_words = [keep.tile([P, G, 2 * NT], U8, name="f_words%d" % n, align_bytes=64) for n in range(NB)]
        f_scales = [keep.tile([P, G, NT], U8, name="f_scales0", align_bytes=64),
                    keep.tile([P, G, N - NT], U8, name="f_scales1", align_bytes=64)]
        g_words = [keep.tile([P, G, 4 * NT], U8, name="g_words%d" % n, align_bytes=64) for n in range(NB)]
        g_scales = [keep.tile([P, G, NT], U8, name="g_scales0", align_bytes=64),
                    keep.tile([P, G, N - NT], U8, name="g_scales1", align_bytes=64)]
        l_raw = keep.tile([P, G, 4, D], BF16, name="l_raw", align_bytes=64)
        l_grp = keep.tile([P, G, D, 4], BF16, name="l_grp", align_bytes=64)
        l_codes = keep.tile([P, G, D], U32, name="l_codes", align_bytes=64)
        l_scales = keep.tile([P, G, D], U8, name="l_scales", align_bytes=64)
        votes = [keep.tile([P, 2, NB, POOL, P], F32, name="votes%d" % i, align_bytes=64) for i in range(MT // 2)]
        halves = [keep.tile([P, 2, NB, 2, P], F32, name="halves%d" % i, align_bytes=64) for i in range(MT // 2)]
        results = [keep.tile([P, 2, 2, NB, P], F32, name="results%d" % i, align_bytes=64) for i in range(MT // 2)]
        ident = keep.tile([P, P], F32, name="ident", align_bytes=64)
        zeros = keep.tile([P, NT], BF16, name="zeros", align_bytes=64)
        warm = keep.tile([P, 1], F32, name="warm", align_bytes=64)

        gw = gain_words.rearrange("g p n t -> p g (n t)")
        fw = field_words.rearrange("g p b -> p g b")
        fs = field_scales.rearrange("g r n -> r g n")
        gs = gain_scales.rearrange("g r n -> r g n")

        def load_words(tile, src, lo, hi):
            nc.sync.dma_start(out=tile[:].bitcast(I32), in_=src[:, :, lo:hi].bitcast(I32))

        def load_scales(tile, src, lo, hi):
            for q in range(4):
                nc.sync.dma_start(out=tile[32 * q : 32 * q + 4, :, :].bitcast(I32),
                                  in_=src[4 * q : 4 * q + 4, :, lo:hi].bitcast(I32))

        nc.vector.memset(f_scales[0][:].bitcast(I32), 0)
        nc.vector.memset(warm[:], 0.0)
        nc.vector.memset(g_scales[0][:].bitcast(I32), 0)
        nc.vector.memset(f_scales[1][:].bitcast(I32), 0)
        nc.vector.memset(g_scales[1][:].bitcast(I32), 0)
        nc.gpsimd.memset(zeros[:], 0.0)
        make_identity(nc, ident[:])
        nc.scalar.activation(out=warm[:], in_=warm[:], func=EXP)

        nc.sync.dma_start(out=x_sb[0][:], in_=x_rows[:, 0:1, :])
        load_scales(f_scales[0], fs, 0, NT)
        nc.sync.dma_start(out=x_sb[1][:], in_=x_rows[:, 1:2, :])
        load_words(f_words[0], fw, 0, 2 * NT)
        load_words(g_words[0], gw, 0, 4 * NT)
        nc.sync.dma_start(out=x_sb[2][:], in_=x_rows[:, 2:4, :])
        load_scales(g_scales[0], gs, 0, NT)
        for i in (3, 4):
            nc.sync.dma_start(out=x_sb[i][:], in_=x_rows[:, 2 * i - 2 : 2 * i, :])
        l_view = w_lin.rearrange("(g p j) w -> p g j w", g=G, j=4)
        nc.sync.dma_start(out=l_raw[:, 0, :, :], in_=l_view[:, 0, :, :])
        load_scales(f_scales[1], fs, NT, N)
        load_scales(g_scales[1], gs, NT, N)
        nc.sync.dma_start(out=l_raw[:, 1, :, :], in_=l_view[:, 1, :, :])
        for n in range(1, NB):
            load_words(f_words[n], fw, 2 * NT * n, 2 * NT * (n + 1))
            load_words(g_words[n], gw, 4 * NT * n, 4 * NT * (n + 1))

        def x_words(m):
            if m < 2:
                return x_sb[m][:, 0, :].bitcast(F32)
            return x_sb[1 + m // 2][:, m % 2, :].bitcast(F32)

        def psum_tile(tag, bufs, shape):
            return psum.tile(shape, F32, name="ps_" + tag, tag=tag, bufs=bufs)

        def transpose(m, g, bank):
            for u in range(2):
                nc.tensor.transpose(bank[:, u, :], x_words(m)[:, 256 * g + u : 256 * (g + 1) : 2], ident[:])

        grouped = {}
        banks = {}

        def transpose_all(m):
            bank = psum_tile("turn", 2, [P, G, 2, P])
            for g in range(G):
                transpose(m, g, bank[:, g, :, :])
            banks[m] = bank

        def copy_words(m, engine):
            pair = m // 2
            if pair not in grouped:
                grouped[pair] = work.tile([P, 2, G, P, 4], BF16, name="grouped", tag="grouped", align_bytes=64)
            dst = grouped[pair][:, m % 2, :, :, :].bitcast(F32)
            engine(out=dst, in_=banks[m][:].rearrange("p g u r -> p g r u"))

        def quantize(m0, count):
            src = grouped[m0 // 2][:, m0 % 2 : m0 % 2 + count, :, :, :]
            nc.vector.quantize_mx(
                out=x_codes[:, m0 : m0 + count, :, :].rearrange("p m g r -> p (m g r)").bitcast(FP8X4),
                scales=x_scales[:, m0 : m0 + count, :, :].rearrange("p m g r -> p (m g r)"),
                in_=src.rearrange("p m g r t -> p (m g r t)"))

        def group_linear(i):
            g, c = divmod(i, 4)
            cols = slice(128 * c, 128 * (c + 1))
            nc.scalar.copy(out=l_grp[:, g, cols, :], in_=l_raw[:, g, :, cols].rearrange("p j w -> p w j"))

        def quantize_linear(g):
            nc.vector.quantize_mx(
                out=l_codes[:, g, :].bitcast(FP8X4), scales=l_scales[:, g, :],
                in_=l_grp[:, g, :, :].rearrange("p w j -> p (w j)"))

        def scale_cols(tiles, n, g):
            if n == 0:
                return tiles[0][:, g, :]
            return tiles[1][:, g, NT * (n - 1) : NT * n]

        def field(n, g):
            return f_words[n][:, g, :].bitcast(FP4X4), scale_cols(f_scales, n, g)

        def gain(n, g):
            return g_words[n][:, g, :].bitcast(FP8X4), scale_cols(g_scales, n, g)

        def product(bank, m, operand):
            for g in range(G):
                codes, scales = operand(g)
                nc.tensor.matmul_mx(
                    out=bank, lhsT=x_codes[:, m, g, :].bitcast(FP8X4), lhsT_scale=x_scales[:, m, g, :],
                    rhs=codes, rhs_scale=scales, start=(g == 0), stop=(g == G - 1))

        rates = {}

        def drive(m, n):
            bank = psum_tile("drive", 3, [P, NT])
            product(bank[:], m, lambda g: field(n, g))
            rates[m, n] = work.tile([P, POOL, P], F32, name="rate", tag="rate", bufs=4, align_bytes=64)
            nc.scalar.activation(out=rates[m, n][:], in_=bank[:].rearrange("p (d j) -> p j d", j=POOL), func=EXP)

        def vote(m, n):
            bank = psum_tile("gain", 3, [P, NT])
            product(bank[:], m, lambda g: gain(n, g))
            nc.vector.tensor_tensor(out=votes[m // 2][:, m % 2, n, :, :], in0=bank[:].rearrange("p (d j) -> p j d", j=POOL),
                                    in1=rates[m, n][:], op=MULT)

        def block(m, n):
            drive(m, n)
            vote(m, n)

        direct_banks = {}

        def direct(m):
            bank = psum_tile("turn", 2, [P, D])
            product(bank[:], m, lambda g: (l_codes[:, g, :].bitcast(FP8X4), l_scales[:, g, :]))
            direct_banks[m] = bank

        def pooled_and_total(m, lo, hi):
            return [results[m // 2][:, i, m % 2, lo:hi, :].rearrange("p n d -> p (n d)") for i in (0, 1)]

        def store(m, lo, hi):
            cols = slice(P * lo, P * hi)
            nc.sync.dma_start(out=out[P * m : P * (m + 1), cols], in_=pooled_and_total(m, lo, hi)[1])

        direct_sb = {}

        def copy_direct(m):
            direct_sb[m] = work.tile([P, D], F32, name="direct_sb", tag="direct_sb", align_bytes=64)
            nc.scalar.copy(out=direct_sb[m][:], in_=direct_banks[m][:])

        def add_copied_direct(m):
            pooled, total = pooled_and_total(m, 0, NB)
            nc.gpsimd.tensor_tensor(out=total, in0=direct_sb[m][:], in1=pooled, op=ADD)
            store(m, 0, NB)

        def add_pairs(m, lo, hi, count=1):
            ms = slice(m % 2, m % 2 + count)
            v = votes[m // 2][:, ms, lo:hi, :, :].rearrange("p m n j d -> p m n (j d)")
            h = halves[m // 2][:, ms, lo:hi, :, :].rearrange("p m n j d -> p m n (j d)")
            nc.vector.tensor_tensor(out=h, in0=v[:, :, :, 0 : 2 * P], in1=v[:, :, :, 2 * P : 4 * P], op=ADD)

        def add_halves(m, lo, hi, count=1):
            ms = slice(m % 2, m % 2 + count)
            h = halves[m // 2][:, ms, lo:hi, :, :]
            nc.vector.tensor_tensor(out=results[m // 2][:, 0, ms, lo:hi, :], in0=h[:, :, :, 0, :], in1=h[:, :, :, 1, :], op=ADD)

        def add_direct(m, lo, hi):
            pooled, total = pooled_and_total(m, lo, hi)
            nc.vector.tensor_tensor(out=total, in0=direct_banks[m][:, P * lo : P * hi], in1=pooled, op=ADD)
            store(m, lo, hi)

        idle = psum_tile("drive", 3, [P, NT])
        for i in range(WARM):
            nc.tensor.matmul(idle[:], lhsT=zeros[:, 0:P], rhs=zeros[:], start=True, stop=True)
        grouped[0] = work.tile([P, 2, G, P, 4], BF16, name="grouped", tag="grouped", align_bytes=64)

        def first_tile(m):
            copies = (nc.vector.tensor_copy, nc.scalar.copy)
            for g in range(G):
                bank = psum_tile("turn" if g == 0 else "gain", 2 if g == 0 else 3, [P, 2, P])
                transpose(m, g, bank[:])
                copies[g](out=grouped[0][:, m, g, :, :].bitcast(F32), in_=bank[:].rearrange("p u r -> p r u"))
            for g in range(G):
                nc.vector.quantize_mx(
                    out=x_codes[:, m, g, :].bitcast(FP8X4), scales=x_scales[:, m, g, :],
                    in_=grouped[0][:, m, g, :, :].rearrange("p r t -> p (r t)"))

        first_tile(0)
        nc.tensor.matmul(idle[:], lhsT=zeros[:, 0:P], rhs=zeros[:], start=True, stop=True)
        first_tile(1)
        drive(0, 0)
        drive(1, 0)
        transpose_all(2)
        transpose_all(3)
        copy_words(2, nc.scalar.copy)
        quantize(2, 1)
        copy_words(3, nc.scalar.copy)
        quantize(3, 1)
        vote(0, 0)
        vote(1, 0)
        for m in range(2, MT):
            block(m, 0)
            if m in (2, 4):
                transpose_all(m + 2)
                transpose_all(m + 3)
                copy_words(m + 2, nc.scalar.copy)
                quantize(m + 2, 1)
                copy_words(m + 3, nc.scalar.copy)
                quantize(m + 3, 1)
            if m >= 4:
                group_linear(m - 4)
            if m % 2 == 0:
                add_pairs(m - 2, 0, 1, 2)
            else:
                add_halves(m - 3, 0, 1, 2)
        last = MT - 1
        for m in range(last):
            block(m, 1)
            if m == 0:
                add_pairs(last - 1, 0, 1, 2)
                group_linear(4)
                group_linear(5)
            else:
                add_pairs(m - 1, 1, 4)
            if m > 2:
                add_halves(m - 1, 1, 4)
                direct(m - 1)
                copy_direct(m - 1)
                add_copied_direct(m - 1)
            block(m, 2)
            if m == 2:
                direct(0)
                copy_direct(0)
                add_copied_direct(0)
            if m == 0:
                add_halves(last - 1, 0, 1, 2)
                quantize_linear(0)
                group_linear(6)
            if m == 1:
                quantize_linear(1)
            if m == 2:
                add_halves(m - 1, 1, 4)
            block(m, 3)
            if m == 0:
                group_linear(7)
            if m == 1:
                add_halves(0, 1, 4)
            if m == 2:
                direct(1)
                copy_direct(1)
                add_copied_direct(1)
            if m == last - 1:
                add_pairs(m, 1, 3)
        block(last, 1)
        add_pairs(last - 1, 3, 4)
        direct(last - 1)
        add_halves(last - 1, 1, 4)
        block(last, 2)
        direct(last)
        add_direct(last - 1, 0, 4)
        add_pairs(last, 1, 3)
        block(last, 3)
        add_halves(last, 1, 3)
        add_pairs(last, 3, 4)
        add_direct(last, 0, 3)
        add_halves(last, 3, 4)
        add_direct(last, 3, 4)
